import numpy as np, ml_dtypes
CORES = [33,38,57,62,81,86,161,166,185,190,209,214]
N = 12
NP, NBK, TK, CAP = 6, 8, 64, 10
DEST = [[9,11,7,10,6,11,8,10],[9,6,11,9,6,6,7,7],[8,8,6,9,11,9,9,8],[11,6,10,7,10,7,8,7],[10,11,11,9,9,11,7,11],[6,10,11,10,8,6,7,6]]
def setup_inputs(rng):
    return {"x": rng.standard_normal((N, 128, NBK * TK), dtype=np.float32).astype(ml_dtypes.bfloat16), "w": (rng.standard_normal((N, 128, 128), dtype=np.float32) / 8).astype(ml_dtypes.bfloat16)}
def setup_inputs_big(rng):
    d = setup_inputs(rng)
    for k in ("x", "w"): d[k] = (d[k].astype(np.float32) * 1024.0).astype(d[k].dtype)
    return d
def setup_inputs_small(rng):
    d = setup_inputs(rng)
    for k in ("x", "w"): d[k] = (d[k].astype(np.float32) * (1 / 1024.0)).astype(d[k].dtype)
    return d
def reference(x, w):
    X, W = x.astype(np.float64), w.astype(np.float64)
    y = np.full((N, 128, CAP * TK), np.nan); n = [0] * N
    for p in range(NP):
        for c in range(NBK):
            q = DEST[p][c]
            y[q][:, TK * n[q]:TK * n[q] + TK] = W[q].T @ np.maximum(W[p].T @ X[p][:, TK * c:TK * c + TK], 0.0)
            n[q] += 1
    return {"y": y.astype(ml_dtypes.bfloat16 if x.dtype != np.float64 else np.float64)}

from concourse.bass import DstId, RemoteDMATransfer
from concourse.mybir import AluOpType

NBANK = 6
PER_CALL = 2

SCRATCH = {
    "wsb": ("sbuf", [128, 128], "bfloat16"),
    "xsb": ("sbuf", [128, 512], "bfloat16"),
    "zero": ("sbuf", [128, 512], "float32"),
    "act": ("sbuf", [128, 640], "bfloat16"),
    "ysb": ("sbuf", [128, 640], "bfloat16"),
}
for _k in range(NBANK):
    SCRATCH["ps%d" % _k] = ("psum", [128, 512], "float32")

SEMAPHORES = (["ld", "zs", "rin", "snt", "st"] + ["a%d" % _k for _k in range(NBANK)]
              + ["mm%d" % _k for _k in range(NBANK)] + ["cp%d" % _k for _k in range(NBANK)])


def _pack(trs):
    by = {}
    for t in trs:
        by.setdefault(len(t["blocks"]), []).append(t)
    calls = []
    for w in sorted(by):
        for i in range(0, len(by[w]), PER_CALL):
            calls.append(by[w][i:i + PER_CALL])
    return calls


def _plan(T, topo):
    dest, cores = T.tables["DEST"], T.cores
    slot, fill = {}, {}
    for p, row in enumerate(dest):
        for c, q in enumerate(row):
            slot[(p, c)] = fill.get(q, 0)
            fill[q] = slot[(p, c)] + 1

    def place(a):
        return (topo.host(a), topo.chip(a))

    direct, handed, via = {}, {}, {}
    for p, row in enumerate(dest):
        src, far = cores[p], {}
        direct[src] = {}
        for c, q in enumerate(row):
            (direct[src] if topo.may_write(src, cores[q]) else far).setdefault(q, []).append((p, c))
        if far:
            f = [cores[r] for r in range(len(dest)) if r != p and place(cores[r]) == place(src)
                 and all(topo.may_write(cores[r], cores[q]) for q in far)][0]
            assert f not in handed
            handed[f], via[src] = sorted(far.items()), f

    senders = {}
    for s, own in direct.items():
        rel = handed.get(s, [])
        best = None
        for af in (0, 1):
            for al in (0, 1):
                if af and not (rel and rel[0][0] in own):
                    continue
                if al and not (rel and rel[-1][0] in own and not (af and len(rel) == 1)):
                    continue
                post, used = [{"q": q, "blocks": list(b)} for q, b in rel], set()
                if af:
                    post[0]["blocks"] = own[rel[0][0]] + post[0]["blocks"]
                    used.add(rel[0][0])
                if al:
                    post[-1]["blocks"] = post[-1]["blocks"] + own[rel[-1][0]]
                    used.add(rel[-1][0])
                early = [{"q": q, "blocks": own[q]} for q in sorted(own) if q not in used]
                key = (len(_pack(post)), len(_pack(early)), len(post) + len(early))
                if best is None or key < best[0]:
                    best = (key, post, early, len(own[rel[0][0]]) if af else 0)
        _, post, early, lead = best
        early_calls, post_calls = _pack(early), _pack(post)
        for pc in post_calls:
            for ec in early_calls:
                if len(pc) < PER_CALL and len(ec) == 1 and len(ec[0]["blocks"]) == len(pc[0]["blocks"]):
                    pc.append(ec[0])
                    early_calls.remove(ec)
                    break
        early_calls.sort(key=lambda cl: sum(len(t["blocks"]) for t in cl))
        calls = []
        if s in via:
            calls.append({"post": False, "trs": [{"to": via[s], "blocks": [b for _, bl in handed[via[s]] for b in bl]}]})
        calls += [{"post": False, "trs": cl} for cl in early_calls] + [{"post": True, "trs": cl} for cl in post_calls]
        col = 0
        for t in post + [t for cl in calls for t in cl["trs"]]:
            if "col" not in t:
                t["col"] = col
                col += len(t["blocks"])
        senders[s] = {"calls": calls, "zone": post[0]["col"] + lead if post else None, "rin": 0}

    receivers = {}
    for s, S in senders.items():
        m = -1
        for cl in S["calls"]:
            for t in cl["trs"]:
                t["dst"] = t["to"] if "to" in t else cores[t["q"]]
                m &= topo.mask(s, t["dst"])
        eng = [e for e in range(m.bit_length()) if (m >> e) & 1]
        for k, cl in enumerate(S["calls"]):
            per = 1
            while per * 2 * len(cl["trs"]) <= len(eng):
                per *= 2
            for i, t in enumerate(cl["trs"]):
                t["neng"] = per
                t["mask"] = sum(1 << e for e in eng[i * per:(i + 1) * per])
                if "to" in t:
                    t["sem"], t["at"] = "rin", senders[t["to"]]["zone"]
                    senders[t["to"]]["rin"] = per
                else:
                    sl = sorted(slot[b] for b in t["blocks"])
                    assert sl == list(range(sl[0], sl[0] + len(sl)))
                    t["at"], t["slots"] = sl[0], [slot[b] for b in t["blocks"]]
                    t["when"] = (k + (1 if cl["post"] else 0), s)
                    receivers.setdefault(t["dst"], []).append(t)
    for chunks in receivers.values():
        chunks.sort(key=lambda t: t["when"])
        for k, t in enumerate(chunks):
            t["sem"] = "a%d" % k
    return senders, receivers


def _sender(g, core, T, topo, S, tk):
    rank, sem = T.rank_of(core), T.sem
    g.sync.dma_start(T.wsb[:, :], T.w[:, :]).then_inc(sem.ld, 16)
    g.scalar.dma_start(T.xsb[:, :], T.x[:, :]).then_inc(sem.ld, 16)
    g.vector.memset(T.zero[:, :], 0.0).then_inc(sem.zs, 1)
    g.tensor.wait_ge(sem.ld, 32)
    g.vector.wait_ge(sem.zs, 1)
    ready = []
    for k, cl in enumerate(S["calls"]):
        mine = sorted((t["col"] + i, c) for t in cl["trs"] for i, (p, c) in enumerate(t["blocks"]) if p == rank)
        ps, n, j = T["ps%d" % k], 0, 0
        while j < len(mine):
            e = j + 1
            while e < len(mine) and mine[e][1] == mine[e - 1][1] + 1:
                e += 1
            g.tensor.matmul(out=ps[:, j * tk:e * tk], lhsT=T.wsb[:, :], rhs=T.xsb[:, mine[j][1] * tk:(mine[e - 1][1] + 1) * tk],
                            start=True, stop=True).then_inc(sem["mm%d" % k], 1)
            n, j = n + 1, e
        if n:
            g.vector.wait_ge(sem["mm%d" % k], n)
        n, j = 0, 0
        while j < len(mine):
            e = j + 1
            while e < len(mine) and mine[e][0] == mine[e - 1][0] + 1:
                e += 1
            g.vector.tensor_tensor(out=T.act[:, mine[j][0] * tk:(mine[e - 1][0] + 1) * tk], in0=ps[:, j * tk:e * tk],
                                   in1=T.zero[:, 0:(e - j) * tk], op=AluOpType.max).then_inc(sem["cp%d" % k], 1)
            n, j = n + 1, e
        ready.append(n)
    sent = 0
    for k, cl in enumerate(S["calls"]):
        if ready[k]:
            g.wait_ge(sem["cp%d" % k], ready[k])
        if cl["post"] and k == min(i for i, c in enumerate(S["calls"]) if c["post"]):
            g.wait_ge(sem.rin, S["rin"])
        trs = []
        for t in cl["trs"]:
            rid, pid = topo.addr(t["dst"], core)
            w = len(t["blocks"]) * tk
            trs.append((T.act[:, t["at"] * tk:t["at"] * tk + w], T.act[:, t["col"] * tk:t["col"] * tk + w],
                        sem[t["sem"]], rid, pid, t["mask"]))
            sent += t["neng"]
        if len(trs) == 1:
            out, src, rs, rid, pid, m = trs[0]
            g.remote_dma(out_ap=out, in_ap=src, remote_sem=rs, local_sem=sem.snt, pid=pid, routing_id=rid, dma_engine_mask=m)
        else:
            g.remote_dma_fused([RemoteDMATransfer(dst_ids=[DstId(rid=rid, pnc=pid)], dma_engine_mask=m, remote_sem=rs,
                                                  src=src, dst=out) for out, src, rs, rid, pid, m in trs], local_sem=sem.snt)
    g.wait_ge(sem.snt, sent)


def _receiver(g, T, chunks, tk):
    sem = T.sem
    g.sync.dma_start(T.wsb[:, :], T.w[:, :]).then_inc(sem.ld, 16)
    g.tensor.wait_ge(sem.ld, 16)
    for k, t in enumerate(chunks):
        ps, at, sl = T["ps%d" % k], t["at"], t["slots"]
        g.tensor.wait_ge(sem[t["sem"]], t["neng"])
        n, j = 0, 0
        while j < len(sl):
            e = j + 1
            while e < len(sl) and sl[e] == sl[e - 1] + 1:
                e += 1
            g.tensor.matmul(out=ps[:, (sl[j] - at) * tk:(sl[e - 1] + 1 - at) * tk], lhsT=T.wsb[:, :],
                            rhs=T.act[:, (at + j) * tk:(at + e) * tk], start=True, stop=True).then_inc(sem["mm%d" % k], 1)
            n, j = n + 1, e
        lo, hi = at * tk, (at + len(sl)) * tk
        g.vector.wait_ge(sem["mm%d" % k], n)
        g.vector.tensor_copy(out=T.ysb[:, lo:hi], in_=ps[:, 0:hi - lo]).then_inc(sem["cp%d" % k], 1)
        dq = g.scalar if k % 2 == 0 else g.sync
        dq.wait_ge(sem["cp%d" % k], 1)
        dq.dma_start(T.y[:, lo:hi], T.ysb[:, lo:hi]).then_inc(sem.st, 16)
    g.wait_ge(sem.st, 16 * len(chunks))


def rank_program(g, core, T, topo):
    if T.rank_of(core) is None:
        return
    senders, receivers = _plan(T, topo)
    tk = T.x.shape[1] // len(T.tables["DEST"][0])
    if core in senders:
        _sender(g, core, T, topo, senders[core], tk)
    elif core in receivers:
        _receiver(g, T, receivers[core], tk)
